import numpy as np
import ml_dtypes


def mxq(x, axis, fmt="e4m3"):
    dtype, down = {"e4m3": (ml_dtypes.float8_e4m3fn, 7), "e5m2": (ml_dtypes.float8_e5m2, 14)}[fmt]
    v = np.moveaxis(np.asarray(x, np.float32).astype(ml_dtypes.bfloat16).astype(np.float64), axis, -1)
    blocks = v.reshape(v.shape[:-1] + (-1, 32))
    amax = np.abs(blocks).max(-1, keepdims=True)
    byte = np.maximum(np.where(amax > 0, np.frexp(amax)[1] - 1 + 127, 0) - down, 1)
    scale = np.exp2(byte - 127.0)
    codes = (blocks / scale).astype(np.float32).astype(dtype).astype(np.float64)
    return np.moveaxis((codes * scale).reshape(v.shape), -1, axis)


WIDE = False


def mx_kscale(k):
    if not WIDE:
        return np.ones(k)
    levels = np.array([30, -30])
    if k % 512:
        return np.exp2(np.random.permutation(np.resize(levels, k // 32))).repeat(32)
    a = np.empty((k // 512, 16))
    for p in range(k // 512):
        a[p, :8] = np.random.permutation(np.resize(levels, 8))
        for g in range(8):
            far = levels[np.abs(levels - a[p, g]) >= 10]
            a[p, g + 8] = far[np.random.randint(len(far))]
    return np.exp2(a.ravel()).repeat(32)


BF16 = ml_dtypes.bfloat16


def bf(x):
    return np.asarray(x, np.float32).astype(BF16)


def f64(x):
    return np.asarray(x).astype(np.float64)


E2M1 = np.array([0.0, 0.5, 1.0, 1.5, 2.0, 3.0, 4.0, 6.0, -0.0, -0.5, -1.0, -1.5, -2.0, -3.0, -4.0, -6.0])


def pack_weight(w, fmt):
    k, n = w.shape
    w = f64(bf(w)).reshape(k // 32, 32, n)
    amax = np.abs(w).max(1)
    if fmt in ("e4m3", "e5m2"):
        byte = np.frexp(amax)[1] - 1 + 127 - (7 if fmt == "e4m3" else 14)
    else:
        mant, ex = np.frexp(amax / 6.0)
        byte = np.where(mant > 0.5, ex, ex - 1) + 127
    byte = np.clip(np.where(amax > 0, byte, 1), 1, 254)
    scaled = (w * np.exp2(127.0 - byte)[:, None, :]).reshape(k, n).astype(np.float32)
    by_word = np.ascontiguousarray(scaled.reshape(k // 512, 128, 4, n).transpose(0, 1, 3, 2))
    if fmt in ("e4m3", "e5m2"):
        words = by_word.astype(ml_dtypes.float8_e4m3fn if fmt == "e4m3" else ml_dtypes.float8_e5m2).view(np.uint8)
    else:
        c = by_word.astype(ml_dtypes.float4_e2m1fn).view(np.uint8) & 0xF
        words = c[..., 0::2] | (c[..., 1::2] << 4)
    return np.ascontiguousarray(words), np.ascontiguousarray(byte.astype(np.uint8).reshape(k // 512, 16, n))


def unpack_weight(words, scales, fmt):
    g, p, n, _ = words.shape
    if fmt in ("e4m3", "e5m2"):
        vals = np.ascontiguousarray(words).view(ml_dtypes.float8_e4m3fn if fmt == "e4m3" else ml_dtypes.float8_e5m2).astype(np.float64)
    else:
        nib = np.empty((g, p, n, 4), np.uint8)
        nib[..., 0::2] = words & 0xF
        nib[..., 1::2] = words >> 4
        vals = E2M1[nib]
    vals = vals * np.repeat(np.exp2(scales.astype(np.float64) - 127.0), 8, axis=1)[..., None]
    return vals.transpose(0, 1, 3, 2).reshape(g * 512, n)


K, M, N = 1536, 1536, 1024


def setup_inputs():
    s = mx_kscale(K)
    G = np.random.standard_t(4, (K, N)) * s[:, None]
    g_words, g_scales = pack_weight(G, "e5m2")
    corr = np.random.standard_normal((K, M)) / np.sqrt(K) / s[:, None]
    return {"g_words": g_words, "g_scales": g_scales,
            "corr": bf(corr),
            "state": bf(np.random.standard_normal((M, N))),
            "step": bf(np.random.standard_normal((M, N))),
            "damp": bf(0.7 + 0.1 * np.random.standard_normal(N)),
            "mix": bf(0.5 + 0.1 * np.random.standard_normal(N))}


def reference(g_words, g_scales, corr, state, step, damp, mix):
    G = unpack_weight(g_words, g_scales, "e5m2")
    d = mxq(f64(corr), 0, "e4m3").T @ G
    new_step = f64(mix) * f64(step) + f64(damp) * d
    new_state = f64(state) + new_step
    return new_state, new_step

from contextlib import ExitStack

import concourse.mybir as mybir
from concourse.masks import make_identity

K, M, N = 1536, 1536, 1024
FLOPS = 2 * K * M * N

F32 = mybir.dt.float32
BF16 = mybir.dt.bfloat16
I32 = mybir.dt.int32
U32 = mybir.dt.uint32
U8 = mybir.dt.uint8
E4M3 = mybir.dt.float8_e4m3fn_x4
E5M2 = mybir.dt.float8_e5m2_x4
ADD = mybir.AluOpType.add
MULT = mybir.AluOpType.mult
COPY = mybir.ActivationFunctionType.Copy

P = 128
KG = K // 512
MB = M // 512
NT = N // P
PAIRS = MB * NT // 2


def tile_contingency_newton_correction_e2_kernel(
    tc, g_words, g_scales, corr, state, step, damp, mix, out_0, out_1
):
    nc = tc.nc
    with ExitStack() as ctx:
        keep = ctx.enter_context(tc.tile_pool(name="keep", bufs=1))
        ring = ctx.enter_context(tc.tile_pool(name="ring", bufs=2))
        psum = ctx.enter_context(tc.psum_pool(name="psum", bufs=2))
        ctx.enter_context(tc.manual_schedule())

        raw = [[keep.tile([P, 4, 512], BF16, name="raw%d%d" % (b, g), align_bytes=64) for g in range(KG)] for b in range(MB)]
        codes = [[keep.tile([P, 512], U32, name="codes%d%d" % (b, g), align_bytes=64) for g in range(KG)] for b in range(MB)]
        scales = [[keep.tile([P, 512], U8, name="scales%d%d" % (b, g), align_bytes=64) for g in range(KG)] for b in range(MB)]
        gw = [[keep.tile([P, 512], U32, name="gw%d%d" % (g, h), align_bytes=64) for h in range(2)] for g in range(KG)]
        gs = keep.tile([P, KG, N], U8, name="gs", align_bytes=64)
        step_sb = [keep.tile([P, 4, N], BF16, name="step%d" % b, align_bytes=64) for b in range(MB)]
        state_sb = [keep.tile([P, 4, N], BF16, name="state%d" % b, align_bytes=64) for b in range(MB)]
        ident_f = keep.tile([P, P], F32, name="ident_f")
        ident_b = keep.tile([P, P], BF16, name="ident_b")
        rows = keep.tile([P, P], BF16, name="rows")
        cols = keep.tile([P, 2 * NT], F32, name="cols")

        nc.vector.memset(rows[:], 0.0)
        nc.vector.memset(gs[:].rearrange("p g n -> p (g n)").bitcast(I32), 0)
        make_identity(nc, ident_b[:])
        make_identity(nc, ident_f[:])
        nc.scalar.dma_start(out=rows[0:NT, :], in_=mix.rearrange("(j p) -> j p", p=P))
        nc.scalar.dma_start(out=rows[NT : 2 * NT, :], in_=damp.rearrange("(j p) -> j p", p=P))
        gsi = gs[:].rearrange("p g n -> p (g n)").bitcast(I32).rearrange("p (g n) -> p g n", g=KG)
        for q in range(4):
            nc.scalar.dma_start(
                out=gsi[32 * q : 32 * q + 4, :, :],
                in_=g_scales[:, 4 * q : 4 * q + 4, :].bitcast(I32).rearrange("g r n -> r g n"),
            )

        def load_corr(b):
            for g in range(KG):
                nc.sync.dma_start(
                    out=raw[b][g][:],
                    in_=corr[512 * g : 512 * g + 512, 512 * b : 512 * b + 512].rearrange("(p j) m -> p j m", j=4),
                )

        def load_rows(tiles, src, b):
            nc.sync.dma_start(out=tiles[b][:], in_=src[512 * b : 512 * b + 512, :].rearrange("(p t) n -> p t n", t=4))

        def load_g(h):
            for g in range(KG):
                nc.sync.dma_start(
                    out=gw[g][h][:].bitcast(I32),
                    in_=g_words[g].rearrange("p n t -> p (n t)")[:, 2048 * h : 2048 * h + 2048].bitcast(I32),
                )

        load_corr(0)
        load_rows(step_sb, step, 0)
        load_g(0)
        load_g(1)
        load_corr(1)
        load_rows(step_sb, step, 1)
        load_rows(state_sb, state, 0)
        load_corr(2)
        load_rows(state_sb, state, 1)
        load_rows(step_sb, step, 2)
        load_rows(state_sb, state, 2)

        grouped = {}

        def interleave(copy, b, g, c0, c1):
            if c0 == 0:
                grouped[b, g] = ring.tile([P, 512, 4], BF16, name="grouped", tag="grouped", bufs=3, align_bytes=64)
            copy(out=grouped[b, g][:, c0:c1, :], in_=raw[b][g][:, :, c0:c1].rearrange("p j c -> p c j"))

        def quantize(b, g):
            nc.vector.quantize_mx(
                out=codes[b][g][:].bitcast(E4M3),
                scales=scales[b][g][:],
                in_=grouped[b, g][:].rearrange("p c j -> p (c j)"),
            )

        u_sb, d_ps, new_t, out_st, out_xt = {}, {}, {}, {}, {}

        def tiles_of(i):
            return i // 4, [2 * (i % 4), 2 * (i % 4) + 1]

        def step_t(i):
            b, js = tiles_of(i)
            u_sb[i] = ring.tile([P, 2, 512], F32, name="u", tag="u", bufs=4)
            banks = []
            for j in js:
                bank = psum.tile([P, 4, P], BF16, name="stp", tag="stp", bufs=2)
                banks.append(bank)
                for t in range(4):
                    nc.tensor.transpose(bank[:, t, :], step_sb[b][:, t, j * P : (j + 1) * P], ident_b[:])
            for k, j in enumerate(js):
                nc.scalar.activation(
                    out=u_sb[i][:, k, :], in_=banks[k][:].rearrange("n t p -> n (t p)"), func=COPY, scale=cols[:, j : j + 1]
                )

        def mx(i):
            b, js = tiles_of(i)
            d_ps[i] = []
            for j in js:
                bank = psum.tile([P, 512], F32, name="d", tag="d", bufs=4)
                d_ps[i].append(bank)
                h, n0 = j // 4, (j % 4) * P
                for g in range(KG):
                    nc.tensor.matmul_mx(
                        out=bank[:],
                        lhsT=gw[g][h][:, n0 : n0 + P].bitcast(E5M2),
                        lhsT_scale=gs[:, g, j * P : (j + 1) * P],
                        rhs=codes[b][g][:].bitcast(E4M3),
                        rhs_scale=scales[b][g][:],
                        start=(g == 0),
                        stop=(g == KG - 1),
                    )

        def combine(i):
            b, js = tiles_of(i)
            new_t[i] = ring.tile([P, 2, 512], F32, name="new_t", tag="new_t", bufs=2)
            for k, j in enumerate(js):
                nc.vector.scalar_tensor_tensor(
                    out=new_t[i][:, k, :].rearrange("n (t p) -> n t p", t=4),
                    in0=d_ps[i][k][:].rearrange("n (p t) -> n t p", t=4),
                    scalar=cols[:, NT + j : NT + j + 1],
                    in1=u_sb[i][:, k, :].rearrange("n (t p) -> n t p", t=4),
                    op0=MULT,
                    op1=ADD,
                )

        def turn_back(i):
            b, js = tiles_of(i)
            if i % 4 == 0:
                out_st[b] = ring.tile([P, 4, N], F32, name="out_st", tag="out_st", bufs=2)
            banks = []
            for k, j in enumerate(js):
                bank = psum.tile([P, 4, P], F32, name="nat", tag="nat", bufs=2)
                banks.append(bank)
                for t in range(4):
                    nc.tensor.transpose(bank[:, t, :], new_t[i][:, k, t * P : (t + 1) * P], ident_f[:])
            for k, j in enumerate(js):
                nc.scalar.copy(out=out_st[b][:, :, j * P : (j + 1) * P], in_=banks[k][:])

        def add_state(i):
            b, js = tiles_of(i)
            if i % 4 == 0:
                out_xt[b] = ring.tile([P, 4, N], F32, name="out_xt", tag="out_xt", bufs=2)
            n = slice(js[0] * P, js[0] * P + 2 * P)
            nc.vector.tensor_tensor(out=out_xt[b][:, :, n], in0=out_st[b][:, :, n], in1=state_sb[b][:, :, n], op=ADD)

        def store(dst, tiles, b, n0, n1):
            nc.sync.dma_start(
                out=dst[512 * b : 512 * b + 512, n0:n1].rearrange("(p t) n -> p t n", t=4), in_=tiles[b][:, :, n0:n1]
            )

        vcopy, scopy = nc.vector.tensor_copy, nc.scalar.copy

        interleave(vcopy, 0, 0, 0, 512)
        interleave(scopy, 0, 1, 0, 512)
        interleave(vcopy, 0, 2, 0, 512)
        quantize(0, 0)
        quantize(0, 1)
        quantize(0, 2)
        turn = psum.tile([P, 4, P], BF16, name="stp", tag="stp", bufs=2)
        nc.tensor.transpose(turn[:, 0, :], rows[:], ident_b[:])
        nc.scalar.copy(out=cols[:], in_=turn[:, 0, 0 : 2 * NT])
        for i in range(3):
            step_t(i)

        extra = {
            1: [(vcopy, 1, 0, 0, 512), (scopy, 1, 1, 0, 256)],
            2: [(vcopy, 1, 2, 0, 512), (scopy, 1, 1, 256, 512), (1, 0)],
            3: [(1, 1), (1, 2)],
            5: [(vcopy, 2, 0, 0, 512), (scopy, 2, 1, 0, 256)],
            6: [(scopy, 2, 1, 256, 512), (2, 0), (vcopy, 2, 2, 0, 512)],
            7: [(2, 1), (2, 2)],
        }
        adds = {3: [0], 4: [1, 2], 5: [3], 6: [4], 7: [5], 8: [6], 9: [7], 10: [8], 11: [9], 12: [10], 13: [11]}
        for i in range(PAIRS + 2):
            if i < PAIRS:
                mx(i)
            if 2 <= i and i + 1 < PAIRS:
                step_t(i + 1)
            if 1 <= i <= PAIRS:
                combine(i - 1)
                turn_back(i - 1)
            for job in extra.get(i, []):
                if len(job) == 2:
                    quantize(*job)
                else:
                    interleave(*job)
            for a in adds.get(i, []):
                add_state(a)
            if i == 5:
                store(out_1, out_st, 0, 0, N)
                store(out_0, out_xt, 0, 0, N)
            if i in (7, 9, 11):
                b, h = (i - 3) // 4, ((i - 3) // 2) % 2
                store(out_1, out_st, b, 512 * h, 512 * h + 512)
                store(out_0, out_xt, b, 512 * h, 512 * h + 512)
            if i >= 12:
                q = i - 10
                store(out_1, out_st, 2, 256 * q, 256 * q + 256)
                store(out_0, out_xt, 2, 256 * q, 256 * q + 256)
